import numpy as np, ml_dtypes
CORES = [5,29,101,125,133,157,229,253]
N = 8
import mx_ref
BF = ml_dtypes.bfloat16
def gentries(a):
    return np.ascontiguousarray(a.reshape(8, 16, -1).transpose(0, 2, 1)).reshape(8, -1)
def gtable(e):
    e = np.asarray(e); return np.ascontiguousarray(e.reshape(8, -1, 16).transpose(0, 2, 1)).reshape(128, -1).astype(np.int32)
def gcols(t, e):
    v = np.concatenate([t.reshape(8, 16, -1, 4), np.zeros((8, 16, 1, 4), BF)], axis=2)
    return np.ascontiguousarray(np.stack([v[g][:, e[g]] for g in range(8)])).reshape(128, -1)
def tile(rs):
    return np.stack(rs, axis=2).reshape(128, -1).astype(BF)
def pick(q, e):
    c = np.concatenate([q[0].reshape(128, -1, 4), np.zeros((128, 1, 4), np.uint8)], axis=1); s = np.concatenate([q[1], np.ones((16, 1), np.uint8)], axis=1)
    return (np.ascontiguousarray(c[:, e].reshape(128, -1)), np.ascontiguousarray(s[:, e]))
def join(*qs):
    return (np.concatenate([q[0] for q in qs], axis=1), np.concatenate([q[1] for q in qs], axis=1))
def put(q, e, v):
    c, s = q[0].reshape(128, -1, 4).copy(), q[1].copy(); c[:, e] = v[0].reshape(128, -1, 4); s[:, e] = v[1]
    return (c.reshape(128, -1), s)
def pk(c, s):
    return (np.ascontiguousarray(c), mx_ref.live(s))
def emit(q):
    return q[0], q[1]
def packed(v, rng):
    q = [mx_ref.quantize(np.ascontiguousarray(v[r])) for r in range(N)]
    return np.stack([a for a, b in q]), np.stack([mx_ref.plane(b, rng) for a, b in q])
def values_of_codes():
    e, c = np.zeros((128, 128, 4), np.float32), np.zeros((128, 2, 4), np.uint8)
    e[np.arange(128), np.arange(128), 0] = 1
    c[:127, :, 0] = np.arange(256).reshape(2, 128).T[:127]
    return mx_ref.matmul(mx_ref.quantize(e.reshape(128, 512).astype(BF)), (c.reshape(128, 8), np.full((16, 2), 127, np.uint8))).T.reshape(-1).astype(np.float64)
CODE_VALUE, SCALE_VALUE = values_of_codes(), 2.0 ** (np.arange(256) - 127.0)
def decode(q):
    return (CODE_VALUE[q[0]].reshape(16, 8, -1, 4) * SCALE_VALUE[q[1]][:, None, :, None] + 0.0).reshape(128, -1).astype(np.float32)
def f(rng, *shape):
    return mx_ref.flush((rng.standard_normal(shape, dtype=np.float32) * np.exp2(rng.integers(-2, 3, shape[:-1] + (1,)))).astype(BF))
def wide(rng, *shape, cols=0):
    v = rng.standard_normal(shape, dtype=np.float32) * np.exp2(rng.integers(-12, 13, shape)).astype(np.float32)
    if cols: v *= np.repeat(np.exp2(rng.integers(-cols, cols + 1, shape[:-2] + (1, shape[-1] // 4))) * (rng.random(shape[:-2] + (1, shape[-1] // 4)) > 0.0625), 4, axis=-1).astype(np.float32)
    return mx_ref.flush(v.astype(BF))
C, HALF = 320, 160
STEP = [4, 1, 2]
def big(v):
    v = v.astype(np.float32)
    v[np.abs(v) < np.float32(2.0 ** -16)] = 0
    return v.astype(BF)
def numbers_of(rng):
    return {"x": big(f(rng, N, 128, 4 * C)), "u": np.array(f(rng, N, 128, 512)), "v": np.array(f(rng, N, 128, 512))}
def lists(rng):
    e = np.tile(np.arange(C), (N, 8, 1))
    o = rng.permuted(e, axis=2)
    m = np.zeros((N, 8, C), np.int64)
    np.put_along_axis(m, o, o[:, :, np.arange(C) ^ 1], axis=2)
    return rng.permuted(e, axis=2), m
def stored(q, m):
    return {"gq": np.stack([gtable(q[r]) for r in range(N)]), "gm": np.stack([gtable(m[r]) for r in range(N)])}
def layers(rng):
    return big(f(rng, N, 128, 2048)).reshape(N, 8, 16, 4, 8, 16, 4)
def no_layers():
    return np.zeros((N, 8, 16, 4, 8, 16, 4), np.float32)
def weights(rng, w):
    c, p = packed(np.ascontiguousarray(w.astype(BF)).reshape(N, 128, 2048), rng)
    return {"wc": c, "ws": p}
def setup_inputs(rng):
    return {**numbers_of(rng), **stored(*lists(rng)), **weights(rng, layers(rng))}
def setup_inputs_ties(rng):
    d = numbers_of(rng)
    o = rng.permutation(N)
    q, m = lists(rng)
    k = rng.integers(-1, 2, (N, 8, C)).astype(np.float32)
    k[o[0], rng.permutation(8)[:4]] = 0
    k[o[1]] = np.where(rng.permutation(8) < 4, 1, -1)[:, None]
    k[o[3]] = np.where(np.arange(C) < HALF, 1, -3)
    for g in range(8):
        a, b, p = rng.permutation(HALF), HALF + rng.permutation(HALF), rng.permutation(HALF)
        q[o[3], g] = np.concatenate([a, b] if g == 0 else [b, a])
        m[o[3], g, :HALF] = HALF + p
        m[o[3], g, HALF + p] = np.arange(HALF)
    x = d["x"].reshape(N, 8, 16, C, 4)
    x[:, :, 0] = 0
    x[:, :, 0, :, 0] = k.astype(BF)
    u = d["u"].reshape(N, 128, 128, 4)
    u[:, :, ::16] = 0
    for h in range(0, 128, 16): u[:, h, h, 0] = 1
    w = layers(rng)
    w[:, :, :, :, :, 0] = 0
    return {"x": x.reshape(N, 128, 4 * C), "u": u.reshape(N, 128, 512), "v": d["v"], **stored(q, m), **weights(rng, w)}
def setup_inputs_near(rng):
    d = numbers_of(rng)
    o = rng.permutation(N) % 2
    k = np.where(o == 0, 2.0 ** -30, 1.0)
    x = np.zeros((N, 8, 16, C, 4))
    s = rng.integers(-1, 2, (N, 8, C)) * k[:, None, None]
    x[:, :, 0, :, 0] = 1.125 * s
    x[:, :, 1, :, 0] = -1.25 * s
    x[:, :, 7, :, 0] = 2.0 ** -30
    x[:, :, 8, :, 0] = 2.0 ** -30
    for r in range(N):
        at = [0, C - 1, int(rng.integers(C)), int(rng.integers(C))]
        for g, j in zip(rng.permutation(8)[:4], at): x[r, g, 0, j, 0] = 2.0 ** 30 * rng.choice([-1.0, 1.0])
    u = d["u"].reshape(N, 128, 128, 4)
    u[:, :, ::16] = 0
    for h in range(0, 128, 16):
        u[:, h, h, 0] = (1.125 * k).astype(np.float32).astype(BF)
        u[:, h + 1, h, 0] = k.astype(np.float32).astype(BF)
        u[:, h + 9, h, 0] = 2.0 ** -30
    w = no_layers()
    for g in range(8):
        w[:, g, 8, 0, g, 8, 0] = 32
        w[:, g, 1, 0, g, 9, 0] = np.where(o == 0, 2.0 ** -9, 2.0 ** -30)
    return {"x": x.astype(np.float32).reshape(N, 128, 4 * C).astype(BF), "u": u.reshape(N, 128, 512), "v": d["v"], **stored(*lists(rng)), **weights(rng, w)}
def setup_inputs_odd(rng):
    d = numbers_of(rng)
    x = (1.0 + (2 * rng.integers(0, 64, (N, 8, 16, C, 4)) + 1) * 2.0 ** -7) * np.exp2(-rng.integers(0, 7, (N, 8, 16, C, 4)).astype(np.float64)) * rng.choice([-1.0, 1.0], (N, 8, 16, C, 4))
    e = rng.choice([-1.0, 1.0], (N, 8, C)) * 2.0 ** -8
    n = rng.integers(0, 2, (N, 8, C))
    x[:, :, 8:] = 0
    x[:, :, 0, :, 0] = 1.96875 * 2.0 ** 8 * rng.choice([-1.0, 1.0], (N, 8, 1))
    x[:, :, 1, :, 0] = np.where(n == 0, 5.0, 7.0) * e
    x[:, :, 8, :, 0] = np.where(n == 0, -4.5, -7.5) * e
    x[:, :, 10, :, 0] = 1.125 * 2.0 ** -2
    u = d["u"].reshape(N, 128, 128, 4)
    u[:, :, ::16] = 0
    for h in range(0, 128, 16):
        u[:, h + 1, h, 0] = 1
        u[:, h + 8, h, 0] = 1
    w = no_layers()
    for g in range(8):
        w[:, g, 10, 0, g, 9, 0] = 1.75 * 2.0 ** 5
        for b in range(4): w[:, g, 10, b, g, 11:, 0] = rng.choice([1.125, 1.5, 2.0], (N, 5)) * 2.0 ** -9
    return {"x": x.astype(np.float32).reshape(N, 128, 4 * C).astype(BF), "u": u.reshape(N, 128, 512), "v": d["v"], **stored(*lists(rng)), **weights(rng, w)}
def setup_inputs_ends(rng):
    d = numbers_of(rng)
    o, e, h = rng.permutation(N) % 4, rng.permutation(N) % 4, rng.permutation(8)
    s = rng.choice([-1.0, 1.0], (N, 128, C, 4))
    s[o == 0] = -1
    s[o == 1] = rng.choice([-1.0, 1.0], (N, 1, C, 1))[o == 1]
    x = s * (0.955 + 0.02 * rng.random((N, 128, C, 4))) * 2.0 ** 30
    x[o == 3] = 2.0 ** -30
    size = np.where(o == 3, 2.0 ** -30, 2.0 ** 30)
    a = np.stack([rng.permutation(8) % 2 * 2.0 - 1.0 for r in range(N)]) * size[:, None]
    u = d["u"].reshape(N, 128, 128, 4)
    u[:, :, ::16] = a.astype(np.float32).astype(BF)[:, None, :, None]
    v = rng.choice([-1.0, 1.0], (N, 128, 512)) * np.where(o % 2 == 0, 2.0 ** 30, 2.0 ** -30)[:, None, None]
    q, m = lists(rng)
    c = np.arange(C)
    q[e == 0], m[e == 0] = c, C - 1 - c
    q[e == 1], m[e == 1] = C - 1 - c, c ^ 1
    q[e == 2], m[e == 2] = (c + 1) % C, (c + HALF) % C
    w = no_layers()
    i = np.arange(16)
    for r in range(N):
        for b in range(4):
            if o[r] < 3:
                for g in h[:3]: w[r, g, i, b, g, i, b] = -0.125
            w[r, h[4], i, b, h[3], i, b] = 2.0 ** 30 if o[r] == 3 else 2.0 ** -30
    return {"x": x.astype(np.float32).reshape(N, 128, 4 * C).astype(BF), "u": u.reshape(N, 128, 512), "v": v.astype(np.float32).astype(BF), **stored(q, m), **weights(rng, w)}
def setup_inputs_spread(rng):
    d = setup_inputs(rng)
    d["x"] = big(wide(rng, N, 128, 4 * C, cols=6))
    return d
def check_inputs(d):
    b = []
    for k in ("x", "u", "v"):
        a = np.abs(d[k].astype(np.float32))
        if not (np.isfinite(a).all() and ((a == 0) | (a >= 2.0 ** -30) & (a <= 2.0 ** 30)).all()): b.append("a value of " + k)
    none, least, most = [emit(mx_ref.quantize(np.full((128, 16), k, np.float32).astype(BF)))[1][0, 0] for k in (0.0, 2.0 ** -30, 2.0 ** 30)]
    c = np.arange(C)
    for r in range(N):
        if not (np.sort(gentries(d["gq"][r]), axis=1) == c).all(): b.append("gq: not each column once in a group")
        m = gentries(d["gm"][r])
        if not ((m >= 0) & (m < C)).all(): b.append("an entry of gm")
        elif not ((np.take_along_axis(m, m, axis=1) == c) & (m != c)).all(): b.append("gm: not pairs")
        if ((d["wc"][r] == 0x7F) | (d["wc"][r] == 0xFF)).any(): b.append("wc: a code that is no number")
        s = mx_ref.live(d["ws"][r])
        if ((s != none) & ((s < least) | (s > most))).any(): b.append("ws: a scale out of range")
        if (((d["wc"][r].reshape(16, 8, 512, 4) & 0x7F) != 0) & (s == none)[:, None, :, None]).any(): b.append("wc: a code other than zero under the scale of zeros")
    return b
def exchange(s, m):
    bit = np.roll(s[::16] > 0, 1, axis=0)
    return np.where(np.take_along_axis(bit, np.minimum(m, np.arange(C)), axis=1), m, np.arange(C))
def reference(x, u, v, gq, gm, wc, ws):
    qu = [mx_ref.quantize(u[r]) for r in range(N)]
    lay = [pk(wc[r], ws[r]) for r in range(N)]
    kept, pair = [gentries(gq[r]) for r in range(N)], [gentries(gm[r]) for r in range(N)]
    now = [x[r] for r in range(N)]
    for step in STEP:
        mid, back, sent = [], [], []
        for r in range(N):
            q, m = kept[r], pair[r]
            a, b = np.zeros((9, C), np.int64), np.zeros((9, C), np.int64)
            go = exchange(mx_ref.matmul(qu[r], mx_ref.quantize(now[r])), m)
            a[0] = np.arange(C)
            for g in range(8): a[g + 1] = q[g][go[g][a[g]]]
            t = ((now[r].astype(np.float32) + gcols(now[r], a[1:]).astype(np.float32)) * np.float32(0.5)).astype(BF)
            qt = mx_ref.quantize(t)
            go = exchange(mx_ref.matmul(qu[r], qt), m)
            inv = np.argsort(q, axis=1)
            b[8] = a[8]
            for g in range(7, -1, -1): b[g] = go[g][inv[g][b[g + 1]]]
            sent.append(mx_ref.quantize(tile([mx_ref.matmul(pick(lay[r], np.arange(128 * k, 128 * k + 128)), qt) * np.float32(0.03125) for k in range(4)])))
            miss = np.take_along_axis(a[:8] != b[:8], np.minimum(m, np.arange(C)), axis=1)
            kept[r] = np.where(miss, np.take_along_axis(q, m, axis=1), q)
            mid.append(t)
            back.append(b[:8])
        now = [(mid[r].astype(np.float32) + gcols(decode(sent[r ^ step]).astype(BF), back[r]).astype(np.float32)).astype(BF) for r in range(N)]
    y, qo = np.zeros((N, 128, C), np.float32), np.zeros((N, 8, C), np.float32)
    oc, osc = np.zeros((N, 128, 4 * C), np.uint8), np.zeros((N, 16, C), np.uint8)
    for r in range(N):
        q = mx_ref.quantize(now[r])
        y[r] = mx_ref.matmul(mx_ref.quantize(v[r]), q)
        qo[r] = kept[r]
        oc[r], osc[r] = emit(q)
    return {"y": y, "qo": qo, "oc": oc, "osc": osc}

from concourse.bass import DstId, RemoteDMATransfer
from concourse.mybir import dt, AluOpType, ActivationFunctionType

C, N = 320, 8
STEP = [4, 1, 2]
OP, AF = AluOpType, ActivationFunctionType

SCRATCH = {}
SEMAPHORES = ["cv", "cs", "ct", "cg", "sent", "rarrq", "rarrs", "rsent"]


def _declare():
    def sb(name, n, d):
        SCRATCH[name] = ("sbuf", [128, n], d)

    def mx(name, n):
        sb(name + "q", n, "float8_e4m3fn_x4")
        sb(name + "s", n, "uint8")
    for r in range(4):
        mx("xm%d" % r, C)
    for r in range(3):
        mx("vm%d" % r, C)
        mx("hm%d" % r, C)
        mx("land%d" % r, C)
        SEMAPHORES.extend(["arr%d" % r, "a8s%d" % r, "ashs%d" % r])
    mx("rel", 160)
    mx("um", 128)
    mx("u2", 128)
    mx("vw", 128)
    mx("wm", 512)
    mx("cm", 256)
    mx("em", 512)
    mx("lm", 128)
    for n in ("ut", "vt", "cpat", "ones", "tl"):
        sb(n, 512, "bfloat16")
    sb("ct", 1024, "bfloat16")
    sb("et", 2048, "bfloat16")
    for n in ("blk", "wmask", "ar", "mr", "n0", "phi0", "phi1", "ee", "pho", "phb", "sg", "tin", "ash", "ta"):
        sb(n, C, "bfloat16")
    for n in ("ra", "rb"):
        sb(n, 2 * C, "bfloat16")
    for n in ("wr0", "wr1", "wr2", "wra", "wrb", "tb"):
        sb(n, 352, "bfloat16")
    sb("xh", 4 * C, "bfloat16")
    sb("dsb", 4 * C, "bfloat16")
    for n in ("rep1", "rep2"):
        sb(n, 320, "bfloat16")
    for n in ("z1", "z2"):
        sb(n, 40, "bfloat16")
    sb("kb", 20, "bfloat16")
    sb("own", 24, "float32")
    for n in ("hso", "mso", "hsb", "msb", "dd", "sm", "ft", "ff"):
        sb(n, 160, "float32")
    for n in ("w16", "wi", "gmf", "kap", "wf"):
        sb(n, 20, "float32")
    for n in ("amb", "b160", "t1", "qf", "yt"):
        sb(n, C, "float32")
    sb("cols", 16, "float32")
    for n in ("gqi", "gmi"):
        sb(n, 20, "int32")
    for n in ("x0", "x1", "x2", "vv", "hh", "xi"):
        sb(n, 4 * C, "bfloat16")
    sb("ints", 24, "int32")
    sb("ul", 8, "uint16")
    for n in ("ql", "ml", "kn", "kxo", "kxb", "aoff", "boff", "a8", "n0l"):
        sb(n, 20, "uint16")
    sb("off", 160, "uint16")
    for n in ("zd1", "zd2"):
        SCRATCH[n] = ("dram", [16, 2, 160], "bfloat16")
    for k in (0, 1, 2, 4, 5, 6, 7):
        SCRATCH["ps%d" % k] = ("psum", [128, 512], "float32")
    SEMAPHORES.extend(["dq", "dm", "dx", "du", "dw", "dv", "zw1", "zr1", "zw2", "zr2", "oend"])


_declare()


def _relays(topo, src, dst):
    if topo.may_write(src, dst):
        return []
    c = [k for k in topo.cores_of(src) if k != src and topo.may_write(k, dst)]
    same = [k for k in c if topo.die(k) == topo.die(src)]
    other = [k for k in c if topo.die(k) != topo.die(src)]
    return [same[0], other[0]]


def _count(mask):
    return bin(mask).count("1")


def V(name, lo, hi, step=1, p0=0, p1=128):
    return (name, lo, hi, step, p0, p1)


def _machine(g, T):
    eng = {"v": g.vector, "s": g.scalar, "t": g.tensor, "g": g, "y": g.sync}
    cnt, log, snap, closed = {}, {}, {}, set()
    known = {q: {} for q in eng}

    def ap(r):
        n, lo, hi, st, p0, p1 = r
        if st == 1:
            return T[n][p0:p1, lo:hi]
        return T[n][p0:p1, lo:hi:st]

    def hit(a, b):
        if a[1] >= b[2] or b[1] >= a[2] or a[4] >= b[5] or b[4] >= a[5]:
            return False
        if a[3] == b[3] and a[3] > 1 and (a[1] - b[1]) % a[3]:
            return False
        return True

    def learn(q, sem, c):
        k = known[q]
        if k.get(sem, 0) >= c:
            return
        k[sem] = c
        for s, v in snap.get((sem, c), {}).items():
            if k.get(s, 0) < v:
                k[s] = v

    def wait(q, sem, c):
        if known[q].get(sem, 0) >= c:
            return
        if sem not in ("cv", "cs", "ct", "cg"):
            c = cnt[sem]
            closed.add(sem)
        eng[q].wait_ge(T.sem[sem], c)
        learn(q, sem, c)

    def norm(r):
        if r[0].startswith("ps"):
            return (r[0], 0, 512, 1, 0, 128)
        return r

    def deps(q, reads, writes):
        need = {}
        for rs, w in ((reads, False), (writes, True)):
            for r in rs:
                r = norm(r)
                ps = r[0].startswith("ps")
                for (o, ow, oq, sem, c) in log.get(r[0], []):
                    if (w or ow or (ps and oq != q)) and hit(r, o):
                        if need.get(sem, 0) < c:
                            need[sem] = c
        own = known[q]
        for sem in sorted(need, key=lambda s: (s == "c" + q, s)):
            if own.get(sem, 0) < need[sem]:
                wait(q, sem, need[sem])

    def note(q, reads, writes, sem):
        c = cnt[sem]
        s = dict(known[q])
        snap[(sem, c)] = s
        for rs, w in ((reads, False), (writes, True)):
            for r in rs:
                r = norm(r)
                old = log.get(r[0], [])
                if w:
                    old = [e for e in old if not (r[1] <= e[0][1] and e[0][2] <= r[2] and r[3] == 1
                                                  and r[4] <= e[0][4] and e[0][5] <= r[5])]
                log[r[0]] = old + [(r, w, q, sem, c)]

    def op(q, fn, reads, writes):
        deps(q, reads, writes)
        sem = "c" + q
        cnt[sem] = cnt.get(sem, 0) + 1
        fn().then_inc(T.sem[sem], 1)
        note(q, reads, writes, sem)

    def dma(q, sem, out, inn, reads, writes):
        deps(q, reads, writes)
        if sem in closed:
            raise ValueError("semaphore " + sem + " was waited for already")
        cnt[sem] = cnt.get(sem, 0) + 16
        eng[q].dma_start(out, inn).then_inc(T.sem[sem], 16)
        note(q, reads, writes, sem)

    def arrived(q, sem, c, writes):
        cnt[sem] = c
        wait(q, sem, c)

    def finish():
        for sem in sorted(cnt):
            if known["g"].get(sem, 0) < cnt[sem]:
                g.wait_ge(T.sem[sem], cnt[sem])

    return {"ap": ap, "op": op, "dma": dma, "deps": deps, "arrived": arrived, "finish": finish, "cnt": cnt, "note": note}


def _relay_program(g, core, T, topo):
    for r in range(N):
        src, dst = T.cores[r], T.cores[r ^ STEP[1]]
        way = _relays(topo, src, dst)
        if core not in way:
            continue
        i = way.index(core)
        a, b = 160 * i, 160 * i + 160
        rid, pid = topo.addr(dst, core)
        m, e = topo.mask(core, dst), len(topo.engines(src, core)) // len(way)
        g.wait_ge(T.sem.rarrq, e)
        g.remote_dma(T.land1q[:, a:b].bitcast(dt.uint8), T.relq[:, 0:160].bitcast(dt.uint8), T.sem.arr1, T.sem.rsent, pid, rid, m)
        g.wait_ge(T.sem.rarrs, e)
        g.remote_dma(T.land1s[:, a:b], T.rels[:, 0:160], T.sem.arr1, T.sem.rsent, pid, rid, m)
        g.wait_ge(T.sem.rsent, 2 * _count(m))


def rank_program(g, core, T, topo):
    rank = T.rank_of(core)
    if rank is None:
        _relay_program(g, core, T, topo)
        return
    M = _machine(g, T)
    ap, op, dma = M["ap"], M["op"], M["dma"]

    def src(inn, off):
        return ap(inn) if off is None else ap(inn).indirect(ap(off))

    def rd(*rs):
        return [r for r in rs if isinstance(r, tuple)]

    def cp(out, inn, off=None):
        op("v", lambda: g.vector.tensor_copy(ap(out), src(inn, off)), rd(inn, off), [out])

    def tt(out, a, b, o, off=None):
        op("v", lambda: g.vector.tensor_tensor(ap(out), src(a, off), ap(b), o), rd(a, b, off), [out])

    def ts(out, a, s1, s2, o0, o1=None, off=None):
        k1 = ap(s1) if isinstance(s1, tuple) else s1
        k2 = ap(s2) if isinstance(s2, tuple) else s2
        if o1 is None:
            op("v", lambda: g.vector.tensor_scalar(ap(out), src(a, off), k1, None, o0), rd(a, s1, off), [out])
        else:
            op("v", lambda: g.vector.tensor_scalar(ap(out), src(a, off), k1, k2, o0, o1), rd(a, s1, s2, off), [out])

    def act(out, inn, func=AF.Copy, scale=1.0, bias=None, off=None):
        k = ap(scale) if isinstance(scale, tuple) else scale
        if bias is None:
            op("s", lambda: g.scalar.activation(ap(out), src(inn, off), func, scale=k), rd(inn, scale, off), [out])
        else:
            op("s", lambda: g.scalar.activation(ap(out), src(inn, off), func, bias=ap(bias), scale=k), rd(inn, scale, bias, off), [out])

    def fill(r, c):
        op("v", lambda: g.vector.memset(ap(r), c), [], [r])

    def tr(out, inn):
        op("v", lambda: g.vector.transpose(ap(out), ap(inn)), [inn], [out])

    def qz(n, lo, hi, inn):
        q, s = V(n + "q", lo, hi), V(n + "s", lo, hi)
        op("v", lambda: g.vector.quantize_mx(ap(q), ap(s), ap(inn)), [inn], [q, s])

    def mm(ps, n, a, alo, b, blo=0):
        aq, as_, bq, bs = V(a + "q", alo, alo + 128), V(a + "s", alo, alo + 128), V(b + "q", blo, blo + n), V(b + "s", blo, blo + n)
        o = V(ps, 0, n)
        op("t", lambda: g.tensor.matmul_mx(ap(o), ap(aq), ap(as_), ap(bq), ap(bs), True, True), [aq, as_, bq, bs], [o])

    def iota(r, pattern, base, cm, f=True):
        if f:
            op("g", lambda: g.iota(ap(r), pattern, base, cm, allow_small_or_imprecise_dtypes=True), [], [r])
        else:
            op("g", lambda: g.iota(ap(r), pattern, base, cm), [], [r])

    def sel(out, inn, pattern, o, base, cm):
        op("g", lambda: g.affine_select(ap(out), ap(inn), pattern, o, 0.0, base, cm), [inn], [out])

    dma("y", "dq", T.gqi[:], T.gq[:], [], [V("gqi", 0, 20)])
    dma("s", "dm", T.gmi[:], T.gm[:], [], [V("gmi", 0, 20)])
    dma("s", "du", T.ut[:], T.u[:], [], [V("ut", 0, 512)])
    dma("y", "dx", T.x0[:], T.x[:], [], [V("x0", 0, 4 * C)])
    dma("y", "dw", T.wmq[:, 0:512].bitcast(dt.uint8), T.wc[:, 0:2048], [], [V("wmq", 0, 512)])
    dma("y", "dw", T.wms[:, 0:512], T.ws[:, 0:512], [], [V("wms", 0, 512)])
    dma("y", "dv", T.vt[:], T.v[:], [], [V("vt", 0, 512)])
    IDENT = V("ra", 0, C)
    pid, l16i, a4i, l32i = [V("ints", k, k + 1) for k in range(4)]
    iota(pid, [[1, 1]], 0, 1, False)
    iota(IDENT, [[1, C]], -160, 0)
    iota(V("blk", 0, C), [[0, 10], [1, 2], [0, 16]], 0, 0)
    iota(V("w16", 0, 20), [[16, 20]], 0, 0)
    iota(V("ints", 8, 16), [[16, 8]], 112, 0, False)

    def col(k):
        return V("cols", k, k + 1)
    L16, A4, L32, L32B, MT, MT2, MTN, KE, KO, C1, C0 = [col(k) for k in range(11)]
    ts(l16i, pid, 15, None, OP.bitwise_and)
    ts(a4i, pid, 3, 12, OP.arith_shift_right, OP.bitwise_and)
    ts(l32i, pid, 31, None, OP.bitwise_and)
    cp(L16, l16i)
    cp(A4, a4i)
    cp(L32, l32i)
    ts(KE, L16, 1.0, None, OP.is_equal)
    ts(KO, L16, 2.0, None, OP.is_equal)
    tt(MT, L16, A4, OP.is_equal)
    tt(C1, KO, KE, OP.subtract)
    ts(C0, KO, -1.0, 1.0, OP.mult, OP.add)
    fill(V("own", 8, 16), 320.0)
    sel(V("own", 16, 24), V("own", 8, 16), [[-16, 8]], OP.is_ge, 0, 1)
    sel(V("own", 0, 8), V("own", 16, 24), [[16, 8]], OP.is_ge, 15, -1)
    iota(V("cpat", 0, 512), [[0, 8], [1, 16], [64, 4]], 0, 0)
    fill(V("ones", 0, 512), 1.0)
    fill(V("phi0", 0, C), 1.0)
    fill(V("tl", 320, 512), 0.0)
    act(V("wmask", 0, C), V("blk", 0, C), AF.Identity, C1, C0)
    act(V("ra", C, 2 * C), IDENT)
    act(V("rb", C, 2 * C), IDENT)
    for n in ("wr0", "wr1", "wr2", "wra", "wrb"):
        fill(V(n, 0, 16), 0.0)
        fill(V(n, 336, 352), 0.0)
    QL, ML, KN, KXO, KXB = [V(n, 0, 20) for n in ("ql", "ml", "kn", "kxo", "kxb")]
    WM = V("wmask", 0, C)
    cp(QL, V("gqi", 0, 20))
    cp(ML, V("gmi", 0, 20))
    cp(V("ar", 0, C), IDENT, QL)
    act(V("mr", 0, C), IDENT, AF.Copy, 1.0, None, ML)
    ts(V("z1", 0, 20), V("gqi", 0, 20), -160.0, None, OP.add)
    tt(V("wr0", 16, 336), V("ar", 0, C), WM, OP.mult, ML)

    def turn(n):
        tr(V("ta", 0, C), V(n, 16, 336))
        tr(V("tb", 0, 352), V(n, 0, 352))

    def entries(out, lo):
        tt(V(out, lo, lo + 20, 2), V("ta", 1, C, 32), V("tb", 17, C, 32), OP.add)
        tt(V(out, lo + 1, lo + 20, 2), V("ta", 18, C, 32), V("tb", 34, 352, 32), OP.add)

    def spread(z, zd, rep, w, rdsem):
        for k in range(8):
            dma("y", w, T[zd][:, :, 20 * k:20 * k + 20], T[z][16 * k:16 * k + 16, 0:40], [V(z, 0, 40, 1, 16 * k, 16 * k + 16)],
                [V(zd, 40 * k, 40 * k + 40)])
        for k in range(8):
            dma("y", rdsem, T[rep][16 * k:16 * k + 16, 0:320], T[zd][:, :, :], [V(zd, 0, 320)], [V(rep, 0, 320, 1, 16 * k, 16 * k + 16)])

    turn("wr0")
    entries("z1", 20)
    spread("z1", "zd1", "rep1", "zw1", "zr1")
    ts(V("ints", 16, 24), V("ints", 8, 16), 127, None, OP.bitwise_and)
    cp(V("ul", 0, 8), V("ints", 16, 24))
    qz("um", 0, 128, V("ut", 0, 512))
    op("v", lambda: g.vector.tensor_copy(T.u2q[:, 0:128].bitcast(dt.uint32), T.umq[:, 0:128].bitcast(dt.uint32).indirect(T.ul[:, 0:8])),
       [V("umq", 0, 128), V("ul", 0, 8)], [V("u2q", 0, 128)])
    op("s", lambda: g.scalar.activation(T.u2s[:, 0:128], T.ums[:, 0:128].indirect(T.ul[:, 0:8]), AF.Copy),
       [V("ums", 0, 128), V("ul", 0, 8)], [V("u2s", 0, 128)])
    qz("xm0", 0, C, V("x0", 0, 4 * C))
    mm("ps0", C, "u2", 0, "xm0")
    cp(V("gmf", 0, 20), V("gmi", 0, 20))
    ts(V("wi", 0, 20), V("w16", 0, 20), L16, None, OP.add)
    tt(V("kap", 0, 20), V("gmf", 0, 20), V("wi", 0, 20), OP.min)
    cp(V("kxo", 0, 20, 2), V("kap", 0, 10))
    cp(V("kxo", 1, 20, 2), V("kap", 10, 20))
    ts(MT2, MT, 2.0, None, OP.mult)
    ts(MTN, MT, -1.0, None, OP.mult)
    act(V("pho", 0, C), V("phi0", 0, C), AF.Copy, MT)
    act(V("phb", 0, C), V("phi0", 0, C), AF.Copy, MT)
    ts(L32B, L32, -16.0, None, OP.add)
    ts(V("ct", 0, 512), V("cpat", 0, 512), L32, None, OP.is_equal)
    ts(V("ct", 512, 1024), V("cpat", 0, 512), L32B, None, OP.is_equal)
    qz("cm", 0, 256, V("ct", 0, 1024))

    def halves(X):
        for b in range(4):
            act(V("xh", C * b, C * b + C), V(X, b, 4 * C, 4), AF.Copy, 0.5)
        act(V("xi", 0, 4 * C), V(X, 0, 4 * C), AF.Copy, 0.5)
    halves("x0")

    def differ(rep):
        A, B = V(rep, 0, 160), V(rep, 160, 320)
        tt(V("dd", 0, 160), B, A, OP.subtract)
        tt(V("sm", 0, 160), B, A, OP.add)

    def tables(H, W):
        for k in range(8):
            o = 4 * (k % 2) + k // 2
            act(V(H, o, 160, 8), V("dd", 20 * k, 20 * k + 20))
            act(V(W, o, 160, 8), V("sm", 20 * k, 20 * k + 20), AF.Identity, 0.5, V("own", k, k + 1))

    def bits(kx, phi):
        ts(V("sg", 0, C), V("ps0", 0, C), 0.0, 0.5, OP.is_gt, OP.subtract)
        tt(V("tin", 0, C), V("sg", 0, C), V(phi, 0, C), OP.mult, kx)
        tr(V("tl", 0, C), V("tin", 0, C))
        qz("lm", 0, 128, V("tl", 0, 512))
        mm("ps1", 128, "cm", 0, "lm")
        mm("ps2", 128, "cm", 128, "lm")

    def places(H, W):
        for h in range(2):
            a, b = 80 * h, 80 * h + 80
            tt(V("ft", a, b), V("ps%d" % (1 + h), 0, 80), V(H, a, b), OP.mult)
        for h in range(2):
            a, b = 80 * h, 80 * h + 80
            tt(V("ff", a, b), V("ft", a, b), V(W, a, b), OP.add)

    def listed(g_):
        k = 4 * (g_ % 2) + g_ // 2
        cp(V("off", 20 * g_, 20 * g_ + 20), V("ff", k, 160, 8))

    def step(a, b, g_):
        o = 20 * g_
        act(V(b, 160, 320), V(a, 0, 2 * C), AF.Copy, 1.0, None, V("off", o + 10, o + 20))
        cp(V(b, 0, 160), V(a, 0, 2 * C), V("off", o, o + 10))

    bits(KXO, "pho")
    for b in range(4):
        sel(V("et", 512 * b, 512 * b + 512), V("ones", 0, 512), [[1, 128], [1000, 4]], OP.is_equal, -1000 * b, -1)
    op("v", lambda: g.vector.tensor_copy(T.n0[:, 0:C].indirect(T.ql[:, 0:20]), ap(IDENT)), [IDENT, QL], [V("n0", 0, C)])
    ts(V("own", 0, 8), V("own", 0, 8), 160.0, None, OP.add)
    differ("rep1")
    tables("hso", "mso")
    tt(V("wr1", 16, 336), V("n0", 0, C), WM, OP.mult)
    turn("wr1")
    entries("z2", 0)
    ts(V("n0l", 0, 20), V("z2", 0, 20), 160.0, None, OP.add)
    tt(V("wr2", 16, 336), V("mr", 0, C), WM, OP.mult, V("n0l", 0, 20))
    turn("wr2")
    entries("z2", 20)
    spread("z2", "zd2", "rep2", "zw2", "zr2")

    for rnd in range(3):
        Y, VV, HH = "x%d" % (1 + rnd % 2), "vv", "hh"
        vm, hm, land = "vm%d" % rnd, "hm%d" % rnd, "land%d" % rnd
        partner = T.cores[rank ^ STEP[rnd]]
        if rnd:
            bits(KXO, "pho")
        places("hso", "mso")
        cur, nxt = "ra", "rb"
        listed(7)
        listed(6)
        for g_ in range(7, 0, -1):
            step(cur, nxt, g_)
            if g_ > 1:
                listed(g_ - 2)
            cur, nxt = nxt, cur
        tt(V("wra", 16, 336), V(cur, 0, 2 * C), WM, OP.mult, V("off", 0, 20))
        turn("wra")
        entries("wf", 0)
        ts(V("aoff", 0, 20), V("wf", 0, 20), 160.0, None, OP.add)
        for b in range(4):
            tt(V(VV, b, 4 * C, 4), V("xh", C * b, C * b + C), V("xi", b, 4 * C, 4), OP.add, V("aoff", 0, 20))
        for k in range(8):
            dma("y", "a8s%d" % rnd, T.a8[16 * k:16 * k + 16, 0:20], T.aoff[112:128, 0:20], [V("aoff", 0, 20, 1, 112, 128)],
                [V("a8", 0, 20, 1, 16 * k, 16 * k + 16)])
        dma("y", "ashs%d" % rnd, T.ash[16:128, 0:C], T.wra[0:112, 16:336], [V("wra", 16, 336, 1, 0, 112)], [V("ash", 0, C, 1, 16, 128)])
        qz(vm, 0, C, V(VV, 0, 4 * C))
        mm("ps0", C, "u2", 0, vm)
        if rnd == 0:
            differ("rep2")
            tables("hsb", "msb")
        for b in range(4):
            mm("ps%d" % (4 + b), C, "wm", 128 * b, vm)
            act(V(HH, b, 4 * C, 4), V("ps%d" % (4 + b), 0, C), AF.Copy, 0.03125)
        if rnd == 0:
            tt(V("kb", 0, 20), V("z2", 0, 20), V("z2", 20, 40), OP.min)
            ts(V("kxb", 0, 20, 2), V("kb", 0, 10), 160.0, None, OP.add)
            ts(V("kxb", 1, 20, 2), V("kb", 10, 20), 160.0, None, OP.add)
            cp(V("ash", 0, C, 1, 0, 16), V("rb", C, 2 * C, 1, 0, 16))
        bits(KXB, "phb")
        if rnd == 0:
            qz("em", 0, 512, V("et", 0, 2048))
            qz("vw", 0, 128, V("vt", 0, 512))
        places("hsb", "msb")
        cur, nxt = "ra", "rb"
        listed(0)
        listed(1)
        for g_ in range(8):
            step(cur, nxt, g_)
            if g_ == 0:
                qz(hm, 0, C, V(HH, 0, 4 * C))
            if g_ < 6:
                listed(g_ + 2)
            if g_ == 0:
                M["deps"]("g", [V(hm + "q", 0, C), V(hm + "s", 0, C)], [])
                hq, hs, lq, ls = T[hm + "q"], T[hm + "s"], T[land + "q"], T[land + "s"]
                way = _relays(topo, core, partner)
                tot = 0
                if not way:
                    rid, p = topo.addr(partner, core)
                    m = topo.mask(core, partner)
                    g.remote_dma(lq[:, 0:C].bitcast(dt.uint8), hq[:, 0:C].bitcast(dt.uint8), T.sem["arr%d" % rnd], T.sem.sent, p, rid, m)
                    g.remote_dma(ls[:, 0:C], hs[:, 0:C], T.sem["arr%d" % rnd], T.sem.sent, p, rid, m)
                    tot, got = 2 * _count(m), 2 * _count(m)
                else:
                    got, fq, fs = 0, [], []
                    for i, k in enumerate(way):
                        a, b = 160 * i, 160 * i + 160
                        rid, p = topo.addr(k, core)
                        e = topo.engines(core, k)
                        n = len(e) // len(way)
                        m = sum(1 << x for x in e[n * i:n * i + n])
                        to = [DstId(rid=rid, pnc=p)]
                        fq.append(RemoteDMATransfer(dst_ids=to, dma_engine_mask=m, remote_sem=T.sem.rarrq,
                                                    src=hq[:, a:b].bitcast(dt.uint8), dst=T.relq[:, 0:160].bitcast(dt.uint8)))
                        fs.append(RemoteDMATransfer(dst_ids=to, dma_engine_mask=m, remote_sem=T.sem.rarrs,
                                                    src=hs[:, a:b], dst=T.rels[:, 0:160]))
                        tot += 2 * n
                    g.remote_dma_fused(fq, local_sem=T.sem.sent)
                    g.remote_dma_fused(fs, local_sem=T.sem.sent)
                    for k in _relays(topo, partner, core):
                        got += 2 * _count(topo.mask(k, core))
                M["cnt"]["sent"] = M["cnt"].get("sent", 0) + tot
            cur, nxt = nxt, cur
        tt(V("wrb", 16, 336), V(cur, 0, C), WM, OP.mult, V("a8", 0, 20))
        turn("wrb")
        entries("wf", 0)
        ts(V("boff", 0, 20), V("wf", 0, 20), 160.0, None, OP.add)
        M["arrived"]("t", "arr%d" % rnd, got, [])
        for b in range(4):
            mm("ps%d" % (4 + b), C, "em", 128 * b, land)
            act(V("dsb", C * b, C * b + C), V("ps%d" % (4 + b), 0, C))
        ph, pn = ("phi0", "phi1") if rnd % 2 == 0 else ("phi1", "phi0")
        tt(V("ee", 0, C), V("wrb", 16, 336), V("ash", 0, C), OP.is_equal)

        def new(b):
            tt(V(Y, b, 4 * C, 4), V("dsb", C * b, C * b + C), V(VV, b, 4 * C, 4), OP.add, V("boff", 0, 20))
        new(0)
        tt(V(pn, 0, C), V(ph, 0, C), V("ee", 0, C), OP.is_equal)
        new(1)
        if rnd < 2:
            act(V("pho", 0, C), V(pn, 0, C), AF.Identity, MT2, MTN, KXO)
            act(V("phb", 0, C), V(pn, 0, C), AF.Identity, MT2, MTN, KXB)
        new(2)
        new(3)
        qz("xm%d" % (rnd + 1), 0, C, V(Y, 0, 4 * C))
        if rnd < 2:
            mm("ps0", C, "u2", 0, "xm%d" % (rnd + 1))
            halves(Y)
        else:
            mm("ps0", C, "vw", 0, "xm3")
            dma("y", "oend", T.oc[:, 0:4 * C], T.xm3q[:, 0:C].bitcast(dt.uint8), [V("xm3q", 0, C)], [])
            act(V("yt", 0, C), V("ps0", 0, C))
            dma("s", "oend", T.y[:], T.yt[:], [V("yt", 0, C)], [])
            for k in range(4):
                dma("y", "oend", T.osc[4 * k:4 * k + 4, 0:C], T.xm3s[32 * k:32 * k + 4, 0:C], [V("xm3s", 0, C)], [])
            cp(KN, V("kap", 0, 20))
            tt(V("amb", 0, C), V("ar", 0, C), V("wr0", 16, 336), OP.subtract)
            tt(V("t1", 0, C), V(pn, 0, C), V("amb", 0, C), OP.mult, KN)
            ts(V("b160", 0, C), V("wr0", 16, 336), 160.0, None, OP.add)
            tt(V("qf", 0, C), V("t1", 0, C), V("b160", 0, C), OP.add)
            dma("y", "oend", T.qo[:], T.qf[0:128:16, 0:C], [V("qf", 0, C)], [])
    M["finish"]()
